import numpy as np
import ml_dtypes


def mxq(x, axis, fmt="e4m3"):
    dtype, down = {"e4m3": (ml_dtypes.float8_e4m3fn, 7), "e5m2": (ml_dtypes.float8_e5m2, 14)}[fmt]
    v = np.moveaxis(np.asarray(x, np.float32).astype(ml_dtypes.bfloat16).astype(np.float64), axis, -1)
    blocks = v.reshape(v.shape[:-1] + (-1, 32))
    amax = np.abs(blocks).max(-1, keepdims=True)
    byte = np.maximum(np.where(amax > 0, np.frexp(amax)[1] - 1 + 127, 0) - down, 1)
    scale = np.exp2(byte - 127.0)
    codes = (blocks / scale).astype(np.float32).astype(dtype).astype(np.float64)
    return np.moveaxis((codes * scale).reshape(v.shape), -1, axis)


WIDE = False


def mx_kscale(k):
    if not WIDE:
        return np.ones(k)
    levels = np.array([10, -10, 5, -5, 0])
    if k % 512:
        return np.exp2(np.random.permutation(np.resize(levels, k // 32))).repeat(32)
    a = np.empty((k // 512, 16))
    for p in range(k // 512):
        a[p, :8] = np.random.permutation(np.resize(levels, 8))
        for g in range(8):
            far = levels[np.abs(levels - a[p, g]) >= 10]
            a[p, g + 8] = far[np.random.randint(len(far))]
    return np.exp2(a.ravel()).repeat(32)


def f64(x):
    return np.asarray(x).astype(np.float64)


def striped(idx):
    return np.tile(idx.reshape(-1, 16).T, (8, 1)).astype(np.uint16)


def unstriped(offs):
    return offs[:16].T.reshape(-1).astype(np.int64)


def striped8(idx):
    return np.concatenate([x.reshape(-1, 16).T for x in idx]).astype(np.uint16)


def runs(offs, k):
    lists = np.stack([offs[16 * r : 16 * r + 16].T.reshape(-1) for r in range(8)]).astype(np.int64)
    return lists[np.arange(k) % 512 // 64]


def pack_weight(w):
    k, n = w.shape
    w = f64(np.asarray(w, np.float32).astype(ml_dtypes.bfloat16)).reshape(k // 32, 32, n)
    amax = np.abs(w).max(1)
    byte = np.clip(np.where(amax > 0, np.frexp(amax)[1] - 1 + 127 - 7, 1), 1, 254)
    scaled = (w * np.exp2(127.0 - byte)[:, None, :]).reshape(k, n).astype(np.float32)
    words = np.ascontiguousarray(scaled.reshape(k // 512, 128, 4, n).transpose(0, 1, 3, 2)).astype(ml_dtypes.float8_e4m3fn).view(np.uint8)
    return words, np.ascontiguousarray(byte.astype(np.uint8).reshape(k // 512, 16, n))


def unpack_weight(words, scales):
    g, p, n, _ = words.shape
    vals = np.ascontiguousarray(words).view(ml_dtypes.float8_e4m3fn).astype(np.float64) * np.repeat(np.exp2(scales.astype(np.float64) - 127.0), 8, axis=1)[..., None]
    return vals.transpose(0, 1, 3, 2).reshape(g * 512, n)


def relu(v):
    return np.maximum(v, 0.0)


K, T, S, V, N, H = 512, 2048, 1024, 512, 512, 512


def setup_inputs():
    n = np.random.standard_normal
    s = mx_kscale(K)[:, None]
    u = mx_kscale(H)
    packed_xT = pack_weight(n((K, T)) * s)
    return {
        "x_words": packed_xT[0],
        "x_scales": packed_xT[1],
        "w1": (n((K, H)) / np.sqrt(K) / s * u).astype(np.float32),
        "w2": (n((H, H)) / np.sqrt(H) / u[:, None] * u).astype(np.float32),
        "res": (2 * n((N, S))).astype(np.float32),
        "w3": (n((H, N)) / np.sqrt(H) / u[:, None]).astype(np.float32),
        "offs": striped(np.random.permutation(T)[:S]),
        "order": striped8(np.stack([np.random.permutation(S) for _ in range(8)])),
        "par": striped8(np.random.randint(0, V, (8, S))),
    }


def reference(x_words, x_scales, w1, w2, res, w3, offs, order, par):
    xq = unpack_weight(x_words, x_scales)[:, unstriped(offs)]
    y = relu(mxq(f64(w1), 0, "e4m3").T @ xq)
    o = y[np.arange(H)[:, None], runs(order, H)]
    z = o.reshape(H, V, 2).max(axis=2)
    h = relu(mxq(f64(w2), 0, "e4m3").T @ mxq(z, 0, "e4m3"))
    z2 = y + h[np.arange(H)[:, None], runs(par, H)]
    return f64(res) + (mxq(f64(w3), 0, "e4m3").T @ mxq(z2, 0, "e4m3"))

@@ -1,0 +1,176 @@
+from contextlib import ExitStack
+
+import concourse.mybir as mybir
+
+K, T, S, V, N, H = 512, 2048, 1024, 512, 512, 512
+FLOPS = 2 * K * H * S + 2 * H * H * V + 2 * H * N * S
+
+F32 = mybir.dt.float32
+BF16 = mybir.dt.bfloat16
+I32 = mybir.dt.int32
+U32 = mybir.dt.uint32
+U16 = mybir.dt.uint16
+U8 = mybir.dt.uint8
+FP8X4 = mybir.dt.float8_e4m3fn_x4
+RELU = mybir.ActivationFunctionType.Relu
+ADD = mybir.AluOpType.add
+MAX = mybir.AluOpType.max
+
+P = 128
+PACK = 4
+BANK = 512
+LIST_ROWS = 16
+
+W1_CHUNKS = (256, 256)
+PICK_CHUNKS = (512, 256, 256)
+POOL_CHUNKS = (512, 256, 256)
+FINE_CHUNKS = (256, 256, 256, 128, 128)
+
+
+def spans(widths):
+    return [slice(sum(widths[:i]), sum(widths[: i + 1])) for i in range(len(widths))]
+
+
+def entries(lists, cols):
+    return lists[:, cols.start // LIST_ROWS : cols.stop // LIST_ROWS]
+
+
+def tile_picked_unet1_relu_p_kernel(tc, x_words, x_scales, w1, w2, res, w3, offs, order, par, out):
+    nc = tc.nc
+    with ExitStack() as ctx:
+        keep = ctx.enter_context(tc.tile_pool(name="keep", bufs=1))
+        psum = ctx.enter_context(tc.psum_pool(name="psum", bufs=8))
+
+        def mx_tiles(name, width):
+            codes = keep.tile([P, width], U32, name=name + "_codes", align_bytes=64)
+            scales = keep.tile([P, width], U8, name=name + "_scales", align_bytes=64)
+            return codes, scales
+
+        def quantize(operand, cols, grouped):
+            codes, scales = operand
+            nc.vector.quantize_mx(out=codes[:, cols].bitcast(FP8X4), scales=scales[:, cols], in_=grouped)
+
+        def product(acc, weights, block, points, cols):
+            rows = slice(block * P, (block + 1) * P)
+            nc.tensor.matmul_mx(
+                out=acc,
+                lhsT=weights[0][:, rows].bitcast(FP8X4),
+                lhsT_scale=weights[1][:, rows],
+                rhs=points[0][:, cols].bitcast(FP8X4),
+                rhs_scale=points[1][:, cols],
+                start=True,
+                stop=True,
+            )
+
+        offs_sb = keep.tile([P, S // LIST_ROWS], U16, name="offs_sb")
+        order_sb = keep.tile([P, S // LIST_ROWS], U16, name="order_sb")
+        par_sb = keep.tile([P, S // LIST_ROWS], U16, name="par_sb")
+        words_all = keep.tile([P, T], U32, name="words_all")
+        scales_all = keep.tile([P, T], U8, name="scales_all")
+
+        nc.vector.memset(scales_all[:].bitcast(I32), 0)
+        nc.sync.dma_start(offs_sb[:], offs)
+        for q in range(4):
+            nc.scalar.dma_start(scales_all[32 * q : 32 * q + 4, :].bitcast(I32), x_scales[0, 4 * q : 4 * q + 4, :].bitcast(I32))
+
+        w1_rows = w1.rearrange("(p j) c -> p j c", j=PACK)
+        w1_raw = []
+        for i, cols in enumerate(spans(W1_CHUNKS)):
+            raw = keep.tile([P, PACK, cols.stop - cols.start], F32, name="w1_raw%d" % i)
+            nc.sync.dma_start(raw[:], w1_rows[:, :, cols])
+            w1_raw.append(raw)
+        nc.sync.dma_start(words_all[:].bitcast(I32), x_words[0].rearrange("p n t -> p (n t)").bitcast(I32))
+        nc.sync.dma_start(order_sb[:], order)
+        w2_raw = keep.tile([P, PACK, H], F32, name="w2_raw")
+        nc.sync.dma_start(w2_raw[:], w2.rearrange("(p j) c -> p j c", j=PACK))
+        nc.sync.dma_start(par_sb[:], par)
+        w3_raw = keep.tile([P, PACK, N], F32, name="w3_raw")
+        nc.sync.dma_start(w3_raw[:], w3.rearrange("(p j) c -> p j c", j=PACK))
+        res_rows = res.rearrange("(b p) s -> p b s", p=P)
+        out_rows = out.rearrange("(b p) s -> p b s", p=P)
+        res_sb = []
+        for i, cols in enumerate(spans(FINE_CHUNKS)):
+            piece = keep.tile([P, N // P, cols.stop - cols.start], F32, name="res%d" % i)
+            nc.sync.dma_start(piece[:], res_rows[:, :, cols])
+            res_sb.append(piece)
+
+        picked = mx_tiles("picked", S)
+        nc.vector.tensor_copy(picked[1][:], scales_all[:].indirect(offs_sb[:]))
+
+        def deal_columns(grouped, raw, cols):
+            ms = slice(cols.start // PACK, cols.stop // PACK)
+            nc.scalar.copy(
+                grouped[:, :, ms, :].rearrange("p t m j -> p m j t"),
+                raw[:].rearrange("p j (m t) -> p m j t", t=PACK),
+            )
+
+        def interleave(engine_copy, grouped, planes):
+            engine_copy(
+                grouped[:].rearrange("p (c i) t -> p c t i", i=PACK),
+                planes[:].rearrange("p t (c i) -> p c t i", i=PACK),
+            )
+
+        w1_grouped = keep.tile([P, PACK, P, PACK], BF16, name="w1_grouped", align_bytes=64)
+        for raw, cols in zip(w1_raw, spans(W1_CHUNKS)):
+            deal_columns(w1_grouped, raw, cols)
+        w1_mx = mx_tiles("w1", H)
+        quantize(w1_mx, slice(0, H), w1_grouped[:].rearrange("p t m j -> p (t m j)"))
+        for cols in spans(PICK_CHUNKS):
+            nc.vector.tensor_copy(picked[0][:, cols], words_all[:].indirect(entries(offs_sb, cols)))
+
+        y = [keep.tile([P, S], F32, name="y%d" % t) for t in range(PACK)]
+        for t in range(PACK):
+            pieces = spans(PICK_CHUNKS if t == 0 else (BANK, BANK))
+            for i, cols in enumerate(pieces):
+                acc = psum.tile([P, cols.stop - cols.start], F32, name="acc")
+                product(acc[:], w1_mx, t, picked, cols)
+                if (t, i) == (0, 2):
+                    nc.vector.tensor_scalar_max(y[t][:, cols], acc[:], 0.0)
+                else:
+                    nc.scalar.activation(y[t][:, cols], acc[:], RELU)
+
+        w2_grouped = keep.tile([P, PACK, P, PACK], BF16, name="w2_grouped", align_bytes=64)
+        deal_columns(w2_grouped, w2_raw, slice(0, H))
+        w2_mx = mx_tiles("w2", H)
+        w3_grouped = keep.tile([P, N, PACK], BF16, name="w3_grouped", align_bytes=64)
+        interleave(nc.scalar.copy, w3_grouped, w3_raw)
+        w3_mx = mx_tiles("w3", N)
+
+        h = [keep.tile([P, V], F32, name="h%d" % t) for t in range(PACK)]
+        z_mx = mx_tiles("z", V)
+        for i, cols in enumerate(spans(POOL_CHUNKS)):
+            width = cols.stop - cols.start
+            coarse = slice(cols.start // 2, cols.stop // 2)
+            ordered = keep.tile([P, PACK, width], BF16, name="ordered%d" % i)
+            for t in range(PACK):
+                nc.vector.tensor_copy(ordered[:, t, :], y[t][:].indirect(entries(order_sb, cols)))
+            pairs = ordered[:].rearrange("p t (c i e) -> p c t i e", i=PACK, e=2)
+            z_grouped = keep.tile([P, width // 2, PACK], BF16, name="z_grouped%d" % i, align_bytes=64)
+            nc.vector.tensor_tensor(z_grouped[:].rearrange("p (c i) t -> p c t i", i=PACK), pairs[:, :, :, :, 0], pairs[:, :, :, :, 1], MAX)
+            if i == 0:
+                quantize(w2_mx, slice(0, H), w2_grouped[:].rearrange("p t m j -> p (t m j)"))
+            quantize(z_mx, coarse, z_grouped[:].rearrange("p v t -> p (v t)"))
+            for t in range(PACK):
+                acc = psum.tile([P, width // 2], F32, name="acc")
+                product(acc[:], w2_mx, t, z_mx, coarse)
+                nc.scalar.activation(h[t][:, coarse], acc[:], RELU)
+        quantize(w3_mx, slice(0, N), w3_grouped[:].rearrange("p c j -> p (c j)"))
+
+        z2_mx = mx_tiles("z2", S)
+        for i, cols in enumerate(spans(FINE_CHUNKS)):
+            width = cols.stop - cols.start
+            z2 = keep.tile([P, PACK, width], F32, name="z2_%d" % i)
+            for t in range(PACK):
+                nc.vector.tensor_tensor(z2[:, t, :], h[t][:].indirect(entries(par_sb, cols)), y[t][:, cols], ADD)
+            z2_grouped = keep.tile([P, width, PACK], BF16, name="z2_grouped%d" % i, align_bytes=64)
+            interleave(nc.scalar.copy, z2_grouped, z2)
+            quantize(z2_mx, cols, z2_grouped[:].rearrange("p s t -> p (s t)"))
+            result = keep.tile([P, N // P, width], F32, name="result%d" % i)
+            per_bank = BANK // width
+            for first in range(0, N // P, per_bank):
+                acc = psum.tile([P, per_bank, width], F32, name="acc")
+                for b in range(per_bank):
+                    product(acc[:, b, :], w3_mx, first + b, z2_mx, cols)
+                blocks = slice(first, first + per_bank)
+                nc.vector.tensor_tensor(result[:, blocks, :], acc[:], res_sb[i][:, blocks, :], ADD)
+            nc.sync.dma_start(out_rows[:, :, cols], result[:])

@@ -23,8 +23,9 @@ LIST_ROWS = 16
 
 W1_CHUNKS = (256, 256)
 PICK_CHUNKS = (512, 256, 256)
-POOL_CHUNKS = (512, 256, 256)
-FINE_CHUNKS = (256, 256, 256, 128, 128)
+POOL_CHUNKS = (512, 512)
+FINE_CHUNKS = (512, 512)
+OUT_PARTS = ((512,), (256, 256))
 
 
 def spans(widths):
@@ -41,8 +42,8 @@ def tile_picked_unet1_relu_p_kernel(tc, x_words, x_scales, w1, w2, res, w3, offs
         keep = ctx.enter_context(tc.tile_pool(name="keep", bufs=1))
         psum = ctx.enter_context(tc.psum_pool(name="psum", bufs=8))
 
-        def mx_tiles(name, width):
-            codes = keep.tile([P, width], U32, name=name + "_codes", align_bytes=64)
+        def mx_tiles(name, width, tag=None):
+            codes = keep.tile([P, width], U32, name=name + "_codes", tag=tag or name + "_codes", align_bytes=64)
             scales = keep.tile([P, width], U8, name=name + "_scales", align_bytes=64)
             return codes, scales
 
@@ -70,8 +71,6 @@ def tile_picked_unet1_relu_p_kernel(tc, x_words, x_scales, w1, w2, res, w3, offs
 
         nc.vector.memset(scales_all[:].bitcast(I32), 0)
         nc.sync.dma_start(offs_sb[:], offs)
-        for q in range(4):
-            nc.scalar.dma_start(scales_all[32 * q : 32 * q + 4, :].bitcast(I32), x_scales[0, 4 * q : 4 * q + 4, :].bitcast(I32))
 
         w1_rows = w1.rearrange("(p j) c -> p j c", j=PACK)
         w1_raw = []
@@ -79,6 +78,9 @@ def tile_picked_unet1_relu_p_kernel(tc, x_words, x_scales, w1, w2, res, w3, offs
             raw = keep.tile([P, PACK, cols.stop - cols.start], F32, name="w1_raw%d" % i)
             nc.sync.dma_start(raw[:], w1_rows[:, :, cols])
             w1_raw.append(raw)
+            if i == 0:
+                for q in range(4):
+                    nc.sync.dma_start(scales_all[32 * q : 32 * q + 4, :].bitcast(I32), x_scales[0, 4 * q : 4 * q + 4, :].bitcast(I32))
         nc.sync.dma_start(words_all[:].bitcast(I32), x_words[0].rearrange("p n t -> p (n t)").bitcast(I32))
         nc.sync.dma_start(order_sb[:], order)
         w2_raw = keep.tile([P, PACK, H], F32, name="w2_raw")
@@ -97,80 +99,97 @@ def tile_picked_unet1_relu_p_kernel(tc, x_words, x_scales, w1, w2, res, w3, offs
         picked = mx_tiles("picked", S)
         nc.vector.tensor_copy(picked[1][:], scales_all[:].indirect(offs_sb[:]))
 
-        def deal_columns(grouped, raw, cols):
+        def deal_columns(engine_copy, grouped, raw, cols):
             ms = slice(cols.start // PACK, cols.stop // PACK)
-            nc.scalar.copy(
-                grouped[:, :, ms, :].rearrange("p t m j -> p m j t"),
-                raw[:].rearrange("p j (m t) -> p m j t", t=PACK),
+            engine_copy(
+                grouped[:, :, ms, :].rearrange("p t m j -> p m t j"),
+                raw.rearrange("p j (m t) -> p m t j", t=PACK),
             )
 
         def interleave(engine_copy, grouped, planes):
-            engine_copy(
-                grouped[:].rearrange("p (c i) t -> p c t i", i=PACK),
-                planes[:].rearrange("p t (c i) -> p c t i", i=PACK),
-            )
+            engine_copy(grouped, planes.rearrange("p t c -> p c t"))
 
         w1_grouped = keep.tile([P, PACK, P, PACK], BF16, name="w1_grouped", align_bytes=64)
-        for raw, cols in zip(w1_raw, spans(W1_CHUNKS)):
-            deal_columns(w1_grouped, raw, cols)
+        deal_columns(nc.vector.tensor_copy, w1_grouped[:], w1_raw[0][:, :, :128], slice(0, 128))
+        deal_columns(nc.scalar.copy, w1_grouped[:], w1_raw[0][:, :, 128:], slice(128, 256))
+        deal_columns(nc.scalar.copy, w1_grouped[:], w1_raw[1][:], slice(256, 512))
         w1_mx = mx_tiles("w1", H)
         quantize(w1_mx, slice(0, H), w1_grouped[:].rearrange("p t m j -> p (t m j)"))
         for cols in spans(PICK_CHUNKS):
             nc.vector.tensor_copy(picked[0][:, cols], words_all[:].indirect(entries(offs_sb, cols)))
 
         y = [keep.tile([P, S], F32, name="y%d" % t) for t in range(PACK)]
-        for t in range(PACK):
-            pieces = spans(PICK_CHUNKS if t == 0 else (BANK, BANK))
-            for i, cols in enumerate(pieces):
-                acc = psum.tile([P, cols.stop - cols.start], F32, name="acc")
-                product(acc[:], w1_mx, t, picked, cols)
-                if (t, i) == (0, 2):
-                    nc.vector.tensor_scalar_max(y[t][:, cols], acc[:], 0.0)
-                else:
-                    nc.scalar.activation(y[t][:, cols], acc[:], RELU)
+        pieces = spans(PICK_CHUNKS)
+        halves = spans((BANK, BANK))
+        steps = [(0, cols) for cols in pieces]
+        steps = steps + [(t, cols) for t in range(1, PACK) for cols in halves]
+        for t, cols in steps:
+            acc = psum.tile([P, cols.stop - cols.start], F32, name="acc")
+            product(acc[:], w1_mx, t, picked, cols)
+            if (t, cols) == (0, pieces[2]):
+                nc.vector.tensor_scalar_max(y[t][:, cols], acc[:], 0.0)
+            else:
+                nc.scalar.activation(y[t][:, cols], acc[:], RELU)
 
-        w2_grouped = keep.tile([P, PACK, P, PACK], BF16, name="w2_grouped", align_bytes=64)
-        deal_columns(w2_grouped, w2_raw, slice(0, H))
+        last = POOL_CHUNKS[-1]
+        late = keep.tile([P, (PACK - 1) * last + PACK * H], BF16, name="late", align_bytes=64)
+        w2_grouped = late[:, (PACK - 1) * last :]
+        early = keep.tile([P, PACK * POOL_CHUNKS[0]], BF16, name="early")
+        ordered_of = (early[:], late[:, : PACK * last])
+        deal_columns(nc.scalar.copy, w2_grouped.rearrange("p (t m j) -> p t m j", t=PACK, j=PACK), w2_raw[:], slice(0, H))
         w2_mx = mx_tiles("w2", H)
-        w3_grouped = keep.tile([P, N, PACK], BF16, name="w3_grouped", align_bytes=64)
-        interleave(nc.scalar.copy, w3_grouped, w3_raw)
-        w3_mx = mx_tiles("w3", N)
+        w3_grouped = keep.tile([P, N, PACK], BF16, name="w3_grouped", tag="w3_then_planes", align_bytes=64)
+        interleave(nc.scalar.copy, w3_grouped[:], w3_raw[:])
 
-        h = [keep.tile([P, V], F32, name="h%d" % t) for t in range(PACK)]
+        h = [keep.tile([P, 2 * V], F32, name="h%d" % t) for t in range(PACK)]
+        for t in range(PACK):
+            nc.vector.memset(h[t][:, V:], 0.0)
         z_mx = mx_tiles("z", V)
         for i, cols in enumerate(spans(POOL_CHUNKS)):
             width = cols.stop - cols.start
             coarse = slice(cols.start // 2, cols.stop // 2)
-            ordered = keep.tile([P, PACK, width], BF16, name="ordered%d" % i)
+            ordered = ordered_of[i]
             for t in range(PACK):
-                nc.vector.tensor_copy(ordered[:, t, :], y[t][:].indirect(entries(order_sb, cols)))
-            pairs = ordered[:].rearrange("p t (c i e) -> p c t i e", i=PACK, e=2)
-            z_grouped = keep.tile([P, width // 2, PACK], BF16, name="z_grouped%d" % i, align_bytes=64)
-            nc.vector.tensor_tensor(z_grouped[:].rearrange("p (c i) t -> p c t i", i=PACK), pairs[:, :, :, :, 0], pairs[:, :, :, :, 1], MAX)
+                nc.vector.tensor_copy(ordered[:, t * width : (t + 1) * width], y[t][:].indirect(entries(order_sb, cols)))
+            pairs = ordered.rearrange("p (t v e) -> p v t e", t=PACK, e=2)
+            z_grouped = keep.tile([P, width // 2, PACK], BF16, name="z_grouped%d" % i, tag="z_grouped%d" % i, align_bytes=64)
+            nc.vector.tensor_tensor(z_grouped[:], pairs[:, :, :, 0], pairs[:, :, :, 1], MAX)
             if i == 0:
-                quantize(w2_mx, slice(0, H), w2_grouped[:].rearrange("p t m j -> p (t m j)"))
+                quantize(w2_mx, slice(0, H), w2_grouped)
             quantize(z_mx, coarse, z_grouped[:].rearrange("p v t -> p (v t)"))
             for t in range(PACK):
                 acc = psum.tile([P, width // 2], F32, name="acc")
                 product(acc[:], w2_mx, t, z_mx, coarse)
-                nc.scalar.activation(h[t][:, coarse], acc[:], RELU)
+                if (t, i) == (0, len(POOL_CHUNKS) - 1):
+                    nc.vector.tensor_scalar_max(h[t][:, coarse], acc[:], 0.0)
+                else:
+                    nc.scalar.activation(h[t][:, coarse], acc[:], RELU)
+        w3_mx = mx_tiles("w3", N, tag="z_grouped%d" % (len(POOL_CHUNKS) - 1))
         quantize(w3_mx, slice(0, N), w3_grouped[:].rearrange("p c j -> p (c j)"))
 
         z2_mx = mx_tiles("z2", S)
+        width = FINE_CHUNKS[0]
+        shared = keep.tile([P, (PACK + 1) * width], F32, name="shared", align_bytes=64)
+        first_planes = keep.tile([P, PACK * width], F32, name="first_planes", tag="w3_then_planes", align_bytes=64)
+        second_grouped = keep.tile([P, PACK * width], BF16, name="second_grouped", align_bytes=64)
+        planes_of = (first_planes[:], shared[:, : PACK * width])
+        grouped_of = (shared[:, (PACK - 1) * width :].bitcast(BF16), second_grouped[:])
         for i, cols in enumerate(spans(FINE_CHUNKS)):
-            width = cols.stop - cols.start
-            z2 = keep.tile([P, PACK, width], F32, name="z2_%d" % i)
+            z2 = planes_of[i].rearrange("p (t s) -> p t s", t=PACK)
             for t in range(PACK):
-                nc.vector.tensor_tensor(z2[:, t, :], h[t][:].indirect(entries(par_sb, cols)), y[t][:, cols], ADD)
-            z2_grouped = keep.tile([P, width, PACK], BF16, name="z2_grouped%d" % i, align_bytes=64)
-            interleave(nc.scalar.copy, z2_grouped, z2)
-            quantize(z2_mx, cols, z2_grouped[:].rearrange("p s t -> p (s t)"))
-            result = keep.tile([P, N // P, width], F32, name="result%d" % i)
-            per_bank = BANK // width
-            for first in range(0, N // P, per_bank):
-                acc = psum.tile([P, per_bank, width], F32, name="acc")
-                for b in range(per_bank):
-                    product(acc[:, b, :], w3_mx, first + b, z2_mx, cols)
-                blocks = slice(first, first + per_bank)
-                nc.vector.tensor_tensor(result[:, blocks, :], acc[:], res_sb[i][:, blocks, :], ADD)
-            nc.sync.dma_start(out_rows[:, :, cols], result[:])
+                nc.vector.tensor_tensor(planes_of[i][:, t * width : (t + 1) * width], h[t][:].indirect(entries(par_sb, cols)), y[t][:, cols], ADD)
+            for part in spans(OUT_PARTS[i]):
+                n = part.stop - part.start
+                flat = grouped_of[i][:, PACK * part.start : PACK * part.stop]
+                interleave(nc.scalar.copy, flat.rearrange("p (s t) -> p s t", t=PACK), z2[:, :, part])
+                where = slice(cols.start + part.start, cols.start + part.stop)
+                quantize(z2_mx, where, flat)
+                per_bank = BANK // n
+                for first in range(0, N // P, per_bank):
+                    blocks = slice(first, first + per_bank)
+                    acc = psum.tile([P, per_bank, n], F32, name="acc")
+                    for b in range(per_bank):
+                        product(acc[:, b, :], w3_mx, first + b, z2_mx, where)
+                    result = keep.tile([P, per_bank, n], F32, name="result%d_%d" % (where.start, first))
+                    nc.vector.tensor_tensor(result[:], acc[:], res_sb[i][:, blocks, part], ADD)
+                    nc.sync.dma_start(out_rows[:, blocks, where], result[:])

from contextlib import ExitStack

import concourse.mybir as mybir

K, T, S, V, N, H = 512, 2048, 1024, 512, 512, 512
FLOPS = 2 * K * H * S + 2 * H * H * V + 2 * H * N * S

F32 = mybir.dt.float32
BF16 = mybir.dt.bfloat16
I32 = mybir.dt.int32
U32 = mybir.dt.uint32
U16 = mybir.dt.uint16
U8 = mybir.dt.uint8
FP8X4 = mybir.dt.float8_e4m3fn_x4
RELU = mybir.ActivationFunctionType.Relu
ADD = mybir.AluOpType.add
MAX = mybir.AluOpType.max

P = 128
PACK = 4
BANK = 512
LIST_ROWS = 16

W1_CHUNKS = (256, 256)
PICK_CHUNKS = (512, 256, 256)
POOL_CHUNKS = (512, 512)
FINE_CHUNKS = (512, 512)
OUT_PARTS = ((512,), (256, 256))


def spans(widths):
    return [slice(sum(widths[:i]), sum(widths[: i + 1])) for i in range(len(widths))]


def entries(lists, cols):
    return lists[:, cols.start // LIST_ROWS : cols.stop // LIST_ROWS]


def tile_picked_unet1_relu_p_kernel(tc, x_words, x_scales, w1, w2, res, w3, offs, order, par, out):
    nc = tc.nc
    with ExitStack() as ctx:
        keep = ctx.enter_context(tc.tile_pool(name="keep", bufs=1))
        psum = ctx.enter_context(tc.psum_pool(name="psum", bufs=8))

        def mx_tiles(name, width, tag=None):
            codes = keep.tile([P, width], U32, name=name + "_codes", tag=tag or name + "_codes", align_bytes=64)
            scales = keep.tile([P, width], U8, name=name + "_scales", align_bytes=64)
            return codes, scales

        def quantize(operand, cols, grouped):
            codes, scales = operand
            nc.vector.quantize_mx(out=codes[:, cols].bitcast(FP8X4), scales=scales[:, cols], in_=grouped)

        def product(acc, weights, block, points, cols):
            rows = slice(block * P, (block + 1) * P)
            nc.tensor.matmul_mx(
                out=acc,
                lhsT=weights[0][:, rows].bitcast(FP8X4),
                lhsT_scale=weights[1][:, rows],
                rhs=points[0][:, cols].bitcast(FP8X4),
                rhs_scale=points[1][:, cols],
                start=True,
                stop=True,
            )

        offs_sb = keep.tile([P, S // LIST_ROWS], U16, name="offs_sb")
        order_sb = keep.tile([P, S // LIST_ROWS], U16, name="order_sb")
        par_sb = keep.tile([P, S // LIST_ROWS], U16, name="par_sb")
        words_all = keep.tile([P, T], U32, name="words_all")
        scales_all = keep.tile([P, T], U8, name="scales_all")

        nc.vector.memset(scales_all[:].bitcast(I32), 0)
        nc.sync.dma_start(offs_sb[:], offs)

        w1_rows = w1.rearrange("(p j) c -> p j c", j=PACK)
        w1_raw = []
        for i, cols in enumerate(spans(W1_CHUNKS)):
            raw = keep.tile([P, PACK, cols.stop - cols.start], F32, name="w1_raw%d" % i)
            nc.sync.dma_start(raw[:], w1_rows[:, :, cols])
            w1_raw.append(raw)
            if i == 0:
                for q in range(4):
                    nc.sync.dma_start(scales_all[32 * q : 32 * q + 4, :].bitcast(I32), x_scales[0, 4 * q : 4 * q + 4, :].bitcast(I32))
        nc.sync.dma_start(words_all[:].bitcast(I32), x_words[0].rearrange("p n t -> p (n t)").bitcast(I32))
        nc.sync.dma_start(order_sb[:], order)
        w2_raw = keep.tile([P, PACK, H], F32, name="w2_raw")
        nc.sync.dma_start(w2_raw[:], w2.rearrange("(p j) c -> p j c", j=PACK))
        nc.sync.dma_start(par_sb[:], par)
        w3_raw = keep.tile([P, PACK, N], F32, name="w3_raw")
        nc.sync.dma_start(w3_raw[:], w3.rearrange("(p j) c -> p j c", j=PACK))
        res_rows = res.rearrange("(b p) s -> p b s", p=P)
        out_rows = out.rearrange("(b p) s -> p b s", p=P)
        res_sb = []
        for i, cols in enumerate(spans(FINE_CHUNKS)):
            piece = keep.tile([P, N // P, cols.stop - cols.start], F32, name="res%d" % i)
            nc.sync.dma_start(piece[:], res_rows[:, :, cols])
            res_sb.append(piece)

        picked = mx_tiles("picked", S)
        nc.vector.tensor_copy(picked[1][:], scales_all[:].indirect(offs_sb[:]))

        def deal_columns(engine_copy, grouped, raw, cols):
            ms = slice(cols.start // PACK, cols.stop // PACK)
            engine_copy(
                grouped[:, :, ms, :].rearrange("p t m j -> p m t j"),
                raw.rearrange("p j (m t) -> p m t j", t=PACK),
            )

        def interleave(engine_copy, grouped, planes):
            engine_copy(grouped, planes.rearrange("p t c -> p c t"))

        w1_grouped = keep.tile([P, PACK, P, PACK], BF16, name="w1_grouped", align_bytes=64)
        deal_columns(nc.vector.tensor_copy, w1_grouped[:], w1_raw[0][:, :, :128], slice(0, 128))
        deal_columns(nc.scalar.copy, w1_grouped[:], w1_raw[0][:, :, 128:], slice(128, 256))
        deal_columns(nc.scalar.copy, w1_grouped[:], w1_raw[1][:], slice(256, 512))
        w1_mx = mx_tiles("w1", H)
        quantize(w1_mx, slice(0, H), w1_grouped[:].rearrange("p t m j -> p (t m j)"))
        for cols in spans(PICK_CHUNKS):
            nc.vector.tensor_copy(picked[0][:, cols], words_all[:].indirect(entries(offs_sb, cols)))

        y = [keep.tile([P, S], F32, name="y%d" % t) for t in range(PACK)]
        pieces = spans(PICK_CHUNKS)
        halves = spans((BANK, BANK))
        steps = [(0, cols) for cols in pieces]
        steps = steps + [(t, cols) for t in range(1, PACK) for cols in halves]
        for t, cols in steps:
            acc = psum.tile([P, cols.stop - cols.start], F32, name="acc")
            product(acc[:], w1_mx, t, picked, cols)
            if (t, cols) == (0, pieces[2]):
                nc.vector.tensor_scalar_max(y[t][:, cols], acc[:], 0.0)
            else:
                nc.scalar.activation(y[t][:, cols], acc[:], RELU)

        last = POOL_CHUNKS[-1]
        late = keep.tile([P, (PACK - 1) * last + PACK * H], BF16, name="late", align_bytes=64)
        w2_grouped = late[:, (PACK - 1) * last :]
        early = keep.tile([P, PACK * POOL_CHUNKS[0]], BF16, name="early")
        ordered_of = (early[:], late[:, : PACK * last])
        deal_columns(nc.scalar.copy, w2_grouped.rearrange("p (t m j) -> p t m j", t=PACK, j=PACK), w2_raw[:], slice(0, H))
        w2_mx = mx_tiles("w2", H)
        w3_grouped = keep.tile([P, N, PACK], BF16, name="w3_grouped", tag="w3_then_planes", align_bytes=64)
        interleave(nc.scalar.copy, w3_grouped[:], w3_raw[:])

        h = [keep.tile([P, 2 * V], F32, name="h%d" % t) for t in range(PACK)]
        for t in range(PACK):
            nc.vector.memset(h[t][:, V:], 0.0)
        z_mx = mx_tiles("z", V)
        for i, cols in enumerate(spans(POOL_CHUNKS)):
            width = cols.stop - cols.start
            coarse = slice(cols.start // 2, cols.stop // 2)
            ordered = ordered_of[i]
            for t in range(PACK):
                nc.vector.tensor_copy(ordered[:, t * width : (t + 1) * width], y[t][:].indirect(entries(order_sb, cols)))
            pairs = ordered.rearrange("p (t v e) -> p v t e", t=PACK, e=2)
            z_grouped = keep.tile([P, width // 2, PACK], BF16, name="z_grouped%d" % i, tag="z_grouped%d" % i, align_bytes=64)
            nc.vector.tensor_tensor(z_grouped[:], pairs[:, :, :, 0], pairs[:, :, :, 1], MAX)
            if i == 0:
                quantize(w2_mx, slice(0, H), w2_grouped)
            quantize(z_mx, coarse, z_grouped[:].rearrange("p v t -> p (v t)"))
            for t in range(PACK):
                acc = psum.tile([P, width // 2], F32, name="acc")
                product(acc[:], w2_mx, t, z_mx, coarse)
                if (t, i) == (0, len(POOL_CHUNKS) - 1):
                    nc.vector.tensor_scalar_max(h[t][:, coarse], acc[:], 0.0)
                else:
                    nc.scalar.activation(h[t][:, coarse], acc[:], RELU)
        w3_mx = mx_tiles("w3", N, tag="z_grouped%d" % (len(POOL_CHUNKS) - 1))
        quantize(w3_mx, slice(0, N), w3_grouped[:].rearrange("p c j -> p (c j)"))

        z2_mx = mx_tiles("z2", S)
        width = FINE_CHUNKS[0]
        shared = keep.tile([P, (PACK + 1) * width], F32, name="shared", align_bytes=64)
        first_planes = keep.tile([P, PACK * width], F32, name="first_planes", tag="w3_then_planes", align_bytes=64)
        second_grouped = keep.tile([P, PACK * width], BF16, name="second_grouped", align_bytes=64)
        planes_of = (first_planes[:], shared[:, : PACK * width])
        grouped_of = (shared[:, (PACK - 1) * width :].bitcast(BF16), second_grouped[:])
        for i, cols in enumerate(spans(FINE_CHUNKS)):
            z2 = planes_of[i].rearrange("p (t s) -> p t s", t=PACK)
            for t in range(PACK):
                nc.vector.tensor_tensor(planes_of[i][:, t * width : (t + 1) * width], h[t][:].indirect(entries(par_sb, cols)), y[t][:, cols], ADD)
            for part in spans(OUT_PARTS[i]):
                n = part.stop - part.start
                flat = grouped_of[i][:, PACK * part.start : PACK * part.stop]
                interleave(nc.scalar.copy, flat.rearrange("p (s t) -> p s t", t=PACK), z2[:, :, part])
                where = slice(cols.start + part.start, cols.start + part.stop)
                quantize(z2_mx, where, flat)
                per_bank = BANK // n
                for first in range(0, N // P, per_bank):
                    blocks = slice(first, first + per_bank)
                    acc = psum.tile([P, per_bank, n], F32, name="acc")
                    for b in range(per_bank):
                        product(acc[:, b, :], w3_mx, first + b, z2_mx, where)
                    result = keep.tile([P, per_bank, n], F32, name="result%d_%d" % (where.start, first))
                    nc.vector.tensor_tensor(result[:], acc[:], res_sb[i][:, blocks, part], ADD)
                    nc.sync.dma_start(out_rows[:, blocks, where], result[:])
